import numpy as np
import ml_dtypes


def mxq(x, axis, fmt="e4m3"):
    dtype, down = {"e4m3": (ml_dtypes.float8_e4m3fn, 7), "e5m2": (ml_dtypes.float8_e5m2, 14)}[fmt]
    v = np.moveaxis(np.asarray(x, np.float32).astype(ml_dtypes.bfloat16).astype(np.float64), axis, -1)
    blocks = v.reshape(v.shape[:-1] + (-1, 32))
    amax = np.abs(blocks).max(-1, keepdims=True)
    byte = np.maximum(np.where(amax > 0, np.frexp(amax)[1] - 1 + 127, 0) - down, 1)
    scale = np.exp2(byte - 127.0)
    codes = (blocks / scale).astype(np.float32).astype(dtype).astype(np.float64)
    return np.moveaxis((codes * scale).reshape(v.shape), -1, axis)


WIDE = False


def mx_kscale(k):
    if not WIDE:
        return np.ones(k)
    levels = np.array([10, -10, 5, -5, 0])
    if k % 512:
        return np.exp2(np.random.permutation(np.resize(levels, k // 32))).repeat(32)
    a = np.empty((k // 512, 16))
    for p in range(k // 512):
        a[p, :8] = np.random.permutation(np.resize(levels, 8))
        for g in range(8):
            far = levels[np.abs(levels - a[p, g]) >= 10]
            a[p, g + 8] = far[np.random.randint(len(far))]
    return np.exp2(a.ravel()).repeat(32)


def f64(x):
    return np.asarray(x).astype(np.float64)


def striped(idx):
    return np.tile(np.asarray(idx).reshape(-1, 16).T, (8, 1)).astype(np.uint16)


def unstriped(offs):
    return offs[:16].T.reshape(-1).astype(np.int64)


E2M1 = np.array([0.0, 0.5, 1.0, 1.5, 2.0, 3.0, 4.0, 6.0, -0.0, -0.5, -1.0, -1.5, -2.0, -3.0, -4.0, -6.0])


def pack_weight(w, fmt):
    k, n = w.shape
    w = f64(np.asarray(w, np.float32).astype(ml_dtypes.bfloat16)).reshape(k // 32, 32, n)
    amax = np.abs(w).max(1)
    if fmt == "e4m3":
        byte = np.frexp(amax)[1] - 1 + 127 - 7
    else:
        mant, ex = np.frexp(amax / 6.0)
        byte = np.where(mant > 0.5, ex, ex - 1) + 127
    byte = np.clip(np.where(amax > 0, byte, 1), 1, 254)
    scaled = (w * np.exp2(127.0 - byte)[:, None, :]).reshape(k, n).astype(np.float32)
    by_word = np.ascontiguousarray(scaled.reshape(k // 512, 128, 4, n).transpose(0, 1, 3, 2))
    if fmt == "e4m3":
        words = by_word.astype(ml_dtypes.float8_e4m3fn).view(np.uint8)
    else:
        c = by_word.astype(ml_dtypes.float4_e2m1fn).view(np.uint8) & 0xF
        words = (c[..., 0::2] | (c[..., 1::2] << 4)).reshape(k // 512, 128, 2 * n)
    return np.ascontiguousarray(words), np.ascontiguousarray(byte.astype(np.uint8).reshape(k // 512, 16, n))


def unpack_weight(words, scales, fmt):
    g, _, n = scales.shape
    words = np.ascontiguousarray(words).reshape(g, 128, n, -1)
    if fmt == "e4m3":
        vals = words.view(ml_dtypes.float8_e4m3fn).astype(np.float64)
    else:
        nib = np.empty((g, 128, n, 4), np.uint8)
        nib[..., 0::2] = words & 0xF
        nib[..., 1::2] = words >> 4
        vals = E2M1[nib]
    vals = vals * np.repeat(np.exp2(scales.astype(np.float64) - 127.0), 8, axis=1)[..., None]
    return vals.transpose(0, 1, 3, 2).reshape(g * 512, n)


D, T, I, Q, E, M, C = 512, 2048, 512, 256, 512, 1024, 512


def setup_inputs():
    n = np.random.standard_normal
    idx = np.random.permutation(T)[:I]
    idx2 = np.random.permutation(T)[:I]
    idx3 = np.random.permutation(M)[:Q]
    fd = mx_kscale(D)
    fi = mx_kscale(I)
    fc = mx_kscale(C)
    ti = np.ones(T)
    ti[idx] = fi
    keysp = pack_weight(n((D, T)) / fd[:, None], "e4m3")
    return {
        "query": (n((D, Q)) * 1.0 / np.sqrt(D) * fd[:, None]).astype(np.float32),
        "keys_words": keysp[0],
        "keys_scales": keysp[1],
        "os": (np.random.uniform(0.02, 0.08, (1, I)) * fi).astype(np.float32),
        "vals": (n((E, T)) / ti).astype(np.float32),
        "wm": (n((C, E)) * 1.0 / np.sqrt(C) * fc[:, None]).astype(np.float32),
        "mstore": (n((C, M)) / fc[:, None]).astype(np.float32),
        "offs": striped(idx),
        "offs2": striped(idx2),
        "offs3": striped(idx3),
    }


def reference(query, keys_words, keys_scales, os, vals, wm, mstore, offs, offs2, offs3):
    idx = unstriped(offs)
    idx2 = unstriped(offs2)
    idx3 = unstriped(offs3)
    keysu = unpack_weight(keys_words, keys_scales, "e4m3")
    queryq = mxq(f64(query), 0, "e4m3")
    a = queryq.T @ keysu
    s = a[:, idx] - a[:, idx2]
    w = np.maximum(s, 0.0)
    wo1 = w * f64(os)
    wt1 = wo1.T
    vt1 = f64(vals)[:, idx].T
    vt1q = mxq(vt1, 0, "e4m3")
    wt1q = mxq(wt1, 0, "e4m3")
    o = vt1q.T @ wt1q
    wmq = mxq(f64(wm), 0, "e4m3")
    mstoreq = mxq(f64(mstore), 0, "e4m3")
    me = wmq.T @ mstoreq
    y = np.maximum(o, me[:, idx3])
    return y

@@ -1,0 +1,229 @@
+from contextlib import ExitStack
+
+import concourse.mybir as mybir
+from concourse.masks import make_identity
+
+D, T, SLOTS, Q, E, M, C = 512, 2048, 512, 256, 512, 1024, 512
+FLOPS = 2 * (Q * D * T + E * SLOTS * Q + E * C * M)
+
+F32 = mybir.dt.float32
+BF16 = mybir.dt.bfloat16
+I32 = mybir.dt.int32
+U32 = mybir.dt.uint32
+U16 = mybir.dt.uint16
+U8 = mybir.dt.uint8
+FP8X4 = mybir.dt.float8_e4m3fn_x4
+COPY = mybir.ActivationFunctionType.Copy
+MAX = mybir.AluOpType.max
+MULT = mybir.AluOpType.mult
+
+P = 128
+PACK = 4
+BANK = 512
+POOL_BYTES = T * 4
+
+
+def tile_attend_difference_memorylarger_lean_kernel(
+    tc, query, keys_words, keys_scales, slot_factor, vals, wm, mstore, offs, offs2, offs3, out
+):
+    nc = tc.nc
+    with ExitStack() as ctx:
+        sb = ctx.enter_context(tc.tile_pool(name="sb", bufs=1))
+        reused = ctx.enter_context(tc.tile_pool(name="reused", bufs=1))
+        ps = ctx.enter_context(tc.psum_pool(name="ps", bufs=1))
+
+        def bank(b, shape):
+            return ps.tile(shape, F32, name="bank%d" % b)
+
+        def load_k_first(name, src):
+            raw = sb.tile([P, PACK, src.shape[1]], F32, name=name)
+            nc.sync.dma_start(out=raw[:], in_=src.rearrange("(p j) w -> p j w", j=PACK))
+            return raw
+
+        def interleave(name, raw):
+            width = raw.shape[2]
+            grouped = sb.tile([P, width * PACK], BF16, name=name, align_bytes=64)
+            nc.vector.tensor_copy(
+                out=grouped[:].rearrange("p (c i j) -> p c j i", i=4, j=PACK),
+                in_=raw[:].rearrange("p j (c i) -> p c j i", i=4),
+            )
+            return grouped
+
+        def mx_tiles(name, width):
+            codes = sb.tile([P, width], U32, name=name + "_codes", align_bytes=64)
+            scales = sb.tile([P, width], U8, name=name + "_scales", align_bytes=64)
+            return codes, scales
+
+        def quantise_into(codes, scales, grouped):
+            nc.vector.quantize_mx(out=codes.bitcast(FP8X4), scales=scales, in_=grouped)
+
+        def quantise(name, grouped):
+            codes, scales = mx_tiles(name, grouped.shape[1] // PACK)
+            quantise_into(codes[:], scales[:], grouped[:])
+            return codes, scales
+
+        def product(dst, left, cols, right_codes, right_scales):
+            nc.tensor.matmul_mx(
+                out=dst, lhsT=left[0][:, cols].bitcast(FP8X4), lhsT_scale=left[1][:, cols],
+                rhs=right_codes.bitcast(FP8X4), rhs_scale=right_scales, start=True, stop=True,
+            )
+
+        def leave_psum(on_vector, dst, src):
+            if on_vector:
+                nc.vector.tensor_copy(out=dst, in_=src)
+            else:
+                nc.scalar.copy(out=dst, in_=src)
+
+        def gather(on_vector, dst, window, offsets):
+            if on_vector:
+                nc.vector.tensor_copy(out=dst, in_=window.indirect(offsets))
+            else:
+                nc.scalar.activation(out=dst, in_=window.indirect(offsets), func=COPY)
+
+        key_scales = sb.tile([P, BANK], U8, name="key_scales", align_bytes=64)
+        nc.vector.memset(key_scales[:].bitcast(I32), 0)
+        query_raw = load_k_first("query_raw", query)
+        scale_words = keys_scales[0].bitcast(I32)
+        for quad in range(4):
+            nc.sync.dma_start(
+                out=key_scales[32 * quad : 32 * quad + 16, :].bitcast(I32),
+                in_=scale_words[4 * quad : 4 * quad + 4, :].rearrange("r (a c) -> a r c", a=4),
+            )
+        key_words = keys_words[0].rearrange("p n t -> p (n t)").bitcast(I32)
+        key_codes = []
+        for half in range(2):
+            codes = sb.tile([P, T // 2], U32, name="key_codes%d" % half, align_bytes=64)
+            nc.sync.dma_start(out=codes[:].bitcast(I32), in_=key_words[:, half * (T // 2) : (half + 1) * (T // 2)])
+            key_codes.append(codes)
+        list1 = sb.tile([P, SLOTS // 16], U16, name="list1")
+        nc.sync.dma_start(out=list1[:], in_=offs)
+        list2 = sb.tile([P, SLOTS // 16], U16, name="list2")
+        nc.sync.dma_start(out=list2[:], in_=offs2)
+        wm_raw = load_k_first("wm_raw", wm)
+        list3 = sb.tile([P, Q // 16], U16, name="list3")
+        nc.sync.dma_start(out=list3[:], in_=offs3)
+        store_raw = [load_k_first("store_raw%d" % h, mstore[:, h * BANK : (h + 1) * BANK]) for h in range(2)]
+        factor = sb.tile([P, PACK], F32, name="factor")
+        nc.sync.dma_start(out=factor[:], in_=slot_factor.rearrange("o (p t) -> (o p) t", t=PACK))
+        val_pool = []
+        for j in range(4):
+            window = reused.tile([P, T], F32, name="val_pool%d" % j, offset=j * POOL_BYTES, align_bytes=64)
+            nc.sync.dma_start(out=window[:], in_=vals[j * P : (j + 1) * P, :])
+            val_pool.append(window)
+
+        ident = sb.tile([P, P], F32, name="ident")
+        make_identity(nc, ident[:])
+
+        query_mx = quantise("query", interleave("query_b", query_raw))
+        scores = [sb.tile([P, T], F32, name="scores%d" % h) for h in range(2)]
+        for h in range(2):
+            for a in range(4):
+                acc = bank(4 * h + a, [P, BANK])
+                product(acc[:], query_mx, slice(h * P, (h + 1) * P),
+                        key_codes[a // 2][:, (a % 2) * BANK : (a % 2 + 1) * BANK], key_scales[4 * a :, :])
+                leave_psum(4 * h + a in (1, 3, 5), scores[h][:, a * BANK : (a + 1) * BANK], acc[:])
+
+        def negated_second(h):
+            second = sb.tile([P, SLOTS], F32, name="second%d" % h)
+            nc.scalar.activation(out=second[:], in_=scores[h][:].indirect(list2[:]), func=COPY, scale=-1.0)
+            return second
+
+        def turn_add(acc, src, opens):
+            for t in range(PACK):
+                nc.tensor.matmul(out=acc[:, t, :], lhsT=src[:, t::PACK], rhs=ident[:], is_transpose=True,
+                                 start=(opens and t == 0), stop=(not opens and t == PACK - 1))
+
+        weights_mx = mx_tiles("weights", Q)
+
+        def weigh(h, diff, grouped):
+            nc.vector.scalar_tensor_tensor(
+                out=grouped[:].rearrange("p (q t) -> p q t", t=PACK),
+                in0=diff[:].rearrange("p t q -> p q t"), scalar=0.0,
+                in1=factor[:].unsqueeze(1).to_broadcast([P, P, PACK]), op0=MAX, op1=MULT,
+            )
+            cols = slice(h * P, (h + 1) * P)
+            quantise_into(weights_mx[0][:, cols], weights_mx[1][:, cols], grouped[:])
+
+        memory = [sb.tile([P, M], F32, name="memory%d" % j) for j in range(4)]
+
+        def remember(h, store_mx, banks):
+            for j in range(4):
+                acc = bank(banks[j], [P, BANK])
+                product(acc[:], wm_mx, slice(j * P, (j + 1) * P), store_mx[0][:], store_mx[1][:])
+                leave_psum(False, memory[j][:, h * BANK : (h + 1) * BANK], acc[:])
+
+        second0 = negated_second(0)
+        diff0 = bank(0, [P, PACK, P])
+        turn_add(diff0, second0, True)
+        first0 = sb.tile([P, SLOTS], F32, name="first0")
+        gather(False, first0[:], scores[0][:], list1[:])
+        turn_add(diff0, first0, False)
+        second1 = negated_second(1)
+
+        wm_mx = quantise("wm", interleave("wm_b", wm_raw))
+        remember(0, quantise("store0", interleave("store_b0", store_raw[0])), (1, 2, 3, 4))
+        diff1 = bank(1, [P, PACK, P])
+        turn_add(diff1, second1, True)
+        remember(1, quantise("store1", interleave("store_b1", store_raw[1])), (5, 6, 7, 2))
+        first1 = sb.tile([P, SLOTS], F32, name="first1", tag="store_raw1")
+        gather(True, first1[:], scores[1][:], list1[:])
+        turn_add(diff1, first1, False)
+        weigh(0, diff0, sb.tile([P, BANK], BF16, name="weights_b0", align_bytes=64))
+
+        def pick(j):
+            listed = sb.tile([P, SLOTS], BF16, name="listed%d" % j)
+            if j < 3:
+                gather(True, listed[:], val_pool[j][:], list1[:])
+            else:
+                gather(True, listed[:, : 16 * 16], val_pool[j][:], list1[:, :16])
+                gather(False, listed[:, 16 * 16 :], val_pool[j][:], list1[:, 16:])
+            pairs = listed[:].bitcast(F32)
+            acc = bank((3, 4, 2, 3)[j], [P, 2, P])
+            for u in range(2):
+                nc.tensor.transpose(acc[:, u, :], pairs[:, u::2], ident[:])
+            turned = sb.tile([P, P * PACK], BF16, name="turned%d" % j, align_bytes=64)
+            nc.scalar.copy(out=turned[:].bitcast(F32).rearrange("p (e u) -> p e u", u=2),
+                           in_=acc[:].rearrange("p u e -> p e u"))
+            return turned
+
+        def read(j, turned):
+            if j < 3:
+                codes = reused.tile([P, P], U32, name="vals_codes%d" % j, offset=(j + 1) * POOL_BYTES, align_bytes=64)
+            else:
+                codes = sb.tile([P, P], U32, name="vals_codes3", align_bytes=64)
+            scales = sb.tile([P, P], U8, name="vals_scales%d" % j, align_bytes=64)
+            quantise_into(codes[:], scales[:], turned[:])
+            acc = bank((0, 5, 6, 7)[j], [P, Q])
+            product(acc[:], (codes, scales), slice(0, P), weights_mx[0][:], weights_mx[1][:])
+            return acc
+
+        def finish(j, acc, recalled):
+            if j < 2:
+                result = reused.tile([P, Q], F32, name="result%d" % j, offset=(j + 2) * POOL_BYTES + 1024, align_bytes=64)
+            else:
+                result = sb.tile([P, Q], F32, name="result%d" % j)
+            nc.vector.tensor_tensor(out=result[:], in0=acc[:], in1=recalled, op=MAX)
+            nc.sync.dma_start(out=out[j * P : (j + 1) * P, :], in_=result[:])
+
+        def recall(j, dst):
+            gather(False, dst, memory[j][:], list3[:])
+            return dst
+
+        early = sb.tile([P, 2, Q], F32, name="early")
+        turned0 = pick(0)
+        weigh(1, diff1, reused.tile([P, BANK], BF16, name="weights_b1", offset=0, align_bytes=64))
+        rec0 = recall(0, early[:, 0, :])
+        rec1 = recall(1, early[:, 1, :])
+        turned1 = pick(1)
+        late = sb.tile([P, 2, Q], F32, name="late", tag="listed1")
+        rec2 = recall(2, late[:, 0, :])
+        rec3 = recall(3, late[:, 1, :])
+        acc0 = read(0, turned0)
+        turned2 = pick(2)
+        finish(0, acc0, rec0)
+        acc1 = read(1, turned1)
+        turned3 = pick(3)
+        acc2 = read(2, turned2)
+        finish(1, acc1, rec1)
+        finish(2, acc2, rec2)
+        finish(3, read(3, turned3), rec3)

@@ -36,13 +36,13 @@ def tile_attend_difference_memorylarger_lean_kernel(
             return ps.tile(shape, F32, name="bank%d" % b)
 
         def load_k_first(name, src):
-            raw = sb.tile([P, PACK, src.shape[1]], F32, name=name)
+            raw = sb.tile([P, PACK, src.shape[1]], F32, name=name, align_bytes=64)
             nc.sync.dma_start(out=raw[:], in_=src.rearrange("(p j) w -> p j w", j=PACK))
             return raw
 
-        def interleave(name, raw):
+        def interleave(name, raw, tag):
             width = raw.shape[2]
-            grouped = sb.tile([P, width * PACK], BF16, name=name, align_bytes=64)
+            grouped = sb.tile([P, width * PACK], BF16, name=name, tag=tag, align_bytes=64)
             nc.vector.tensor_copy(
                 out=grouped[:].rearrange("p (c i j) -> p c j i", i=4, j=PACK),
                 in_=raw[:].rearrange("p j (c i) -> p c j i", i=4),
@@ -95,16 +95,16 @@ def tile_attend_difference_memorylarger_lean_kernel(
             codes = sb.tile([P, T // 2], U32, name="key_codes%d" % half, align_bytes=64)
             nc.sync.dma_start(out=codes[:].bitcast(I32), in_=key_words[:, half * (T // 2) : (half + 1) * (T // 2)])
             key_codes.append(codes)
-        list1 = sb.tile([P, SLOTS // 16], U16, name="list1")
-        nc.sync.dma_start(out=list1[:], in_=offs)
         list2 = sb.tile([P, SLOTS // 16], U16, name="list2")
         nc.sync.dma_start(out=list2[:], in_=offs2)
+        list1 = sb.tile([P, SLOTS // 16], U16, name="list1")
+        nc.sync.dma_start(out=list1[:], in_=offs)
         wm_raw = load_k_first("wm_raw", wm)
         list3 = sb.tile([P, Q // 16], U16, name="list3")
         nc.sync.dma_start(out=list3[:], in_=offs3)
-        store_raw = [load_k_first("store_raw%d" % h, mstore[:, h * BANK : (h + 1) * BANK]) for h in range(2)]
         factor = sb.tile([P, PACK], F32, name="factor")
         nc.sync.dma_start(out=factor[:], in_=slot_factor.rearrange("o (p t) -> (o p) t", t=PACK))
+        store_raw = [load_k_first("store_raw%d" % h, mstore[:, h * BANK : (h + 1) * BANK]) for h in range(2)]
         val_pool = []
         for j in range(4):
             window = reused.tile([P, T], F32, name="val_pool%d" % j, offset=j * POOL_BYTES, align_bytes=64)
@@ -114,7 +114,7 @@ def tile_attend_difference_memorylarger_lean_kernel(
         ident = sb.tile([P, P], F32, name="ident")
         make_identity(nc, ident[:])
 
-        query_mx = quantise("query", interleave("query_b", query_raw))
+        query_mx = quantise("query", interleave("query_b", query_raw, "query_b"))
         scores = [sb.tile([P, T], F32, name="scores%d" % h) for h in range(2)]
         for h in range(2):
             for a in range(4):
@@ -141,16 +141,19 @@ def tile_attend_difference_memorylarger_lean_kernel(
                 in0=diff[:].rearrange("p t q -> p q t"), scalar=0.0,
                 in1=factor[:].unsqueeze(1).to_broadcast([P, P, PACK]), op0=MAX, op1=MULT,
             )
+            return grouped
+
+        def quantise_weights(h, grouped):
             cols = slice(h * P, (h + 1) * P)
             quantise_into(weights_mx[0][:, cols], weights_mx[1][:, cols], grouped[:])
 
-        memory = [sb.tile([P, M], F32, name="memory%d" % j) for j in range(4)]
+        memory = [sb.tile([P, M], F32, name="memory%d" % j, align_bytes=64) for j in range(4)]
 
-        def remember(h, store_mx, banks):
+        def remember(h, store_mx, banks, on_vector):
             for j in range(4):
                 acc = bank(banks[j], [P, BANK])
                 product(acc[:], wm_mx, slice(j * P, (j + 1) * P), store_mx[0][:], store_mx[1][:])
-                leave_psum(False, memory[j][:, h * BANK : (h + 1) * BANK], acc[:])
+                leave_psum(j in on_vector, memory[j][:, h * BANK : (h + 1) * BANK], acc[:])
 
         second0 = negated_second(0)
         diff0 = bank(0, [P, PACK, P])
@@ -159,26 +162,28 @@ def tile_attend_difference_memorylarger_lean_kernel(
         gather(False, first0[:], scores[0][:], list1[:])
         turn_add(diff0, first0, False)
         second1 = negated_second(1)
+        first1 = sb.tile([P, SLOTS], F32, name="first1")
+        gather(False, first1[:], scores[1][:], list1[:])
 
-        wm_mx = quantise("wm", interleave("wm_b", wm_raw))
-        remember(0, quantise("store0", interleave("store_b0", store_raw[0])), (1, 2, 3, 4))
-        diff1 = bank(1, [P, PACK, P])
-        turn_add(diff1, second1, True)
-        remember(1, quantise("store1", interleave("store_b1", store_raw[1])), (5, 6, 7, 2))
-        first1 = sb.tile([P, SLOTS], F32, name="first1", tag="store_raw1")
-        gather(True, first1[:], scores[1][:], list1[:])
-        turn_add(diff1, first1, False)
-        weigh(0, diff0, sb.tile([P, BANK], BF16, name="weights_b0", align_bytes=64))
+        wm_mx = quantise("wm", interleave("wm_b", wm_raw, "staged"))
+        remember(0, quantise("store0", interleave("store_b0", store_raw[0], "staged")), (1, 2, 3, 4), ())
+        store_b1 = interleave("store_b1", store_raw[1], "staged")
+        weights_b0 = weigh(0, diff0, sb.tile([P, BANK], BF16, name="weights_b0", tag="store_raw1", align_bytes=64))
+        remember(1, quantise("store1", store_b1), (5, 6, 7, 2), ())
+        quantise_weights(0, weights_b0)
 
         def pick(j):
-            listed = sb.tile([P, SLOTS], BF16, name="listed%d" % j)
+            if j < 3:
+                listed = sb.tile([P, SLOTS], BF16, name="listed%d" % j, tag=("staged", "store_raw1", "memory0")[j], align_bytes=64)
+            else:
+                listed = reused.tile([P, SLOTS], BF16, name="listed3", offset=2 * POOL_BYTES + 1024, align_bytes=64)
             if j < 3:
                 gather(True, listed[:], val_pool[j][:], list1[:])
             else:
                 gather(True, listed[:, : 16 * 16], val_pool[j][:], list1[:, :16])
                 gather(False, listed[:, 16 * 16 :], val_pool[j][:], list1[:, 16:])
             pairs = listed[:].bitcast(F32)
-            acc = bank((3, 4, 2, 3)[j], [P, 2, P])
+            acc = bank((3, 1, 3, 1)[j], [P, 2, P])
             for u in range(2):
                 nc.tensor.transpose(acc[:, u, :], pairs[:, u::2], ident[:])
             turned = sb.tile([P, P * PACK], BF16, name="turned%d" % j, align_bytes=64)
@@ -186,44 +191,55 @@ def tile_attend_difference_memorylarger_lean_kernel(
                            in_=acc[:].rearrange("p u e -> p e u"))
             return turned
 
-        def read(j, turned):
+        def quantise_vals(j, turned):
             if j < 3:
-                codes = reused.tile([P, P], U32, name="vals_codes%d" % j, offset=(j + 1) * POOL_BYTES, align_bytes=64)
+                codes = reused.tile([P, P], U32, name="vals_codes%d" % j, offset=(2 * POOL_BYTES + 2048, 2 * POOL_BYTES, 3 * POOL_BYTES)[j], align_bytes=64)
             else:
                 codes = sb.tile([P, P], U32, name="vals_codes3", align_bytes=64)
             scales = sb.tile([P, P], U8, name="vals_scales%d" % j, align_bytes=64)
             quantise_into(codes[:], scales[:], turned[:])
-            acc = bank((0, 5, 6, 7)[j], [P, Q])
-            product(acc[:], (codes, scales), slice(0, P), weights_mx[0][:], weights_mx[1][:])
+            return codes, scales
+
+        def read(j, vals_mx):
+            acc = bank((0, 4, 6, 7)[j], [P, Q])
+            product(acc[:], vals_mx, slice(0, P), weights_mx[0][:], weights_mx[1][:])
             return acc
 
         def finish(j, acc, recalled):
             if j < 2:
-                result = reused.tile([P, Q], F32, name="result%d" % j, offset=(j + 2) * POOL_BYTES + 1024, align_bytes=64)
+                result = reused.tile([P, Q], F32, name="result%d" % j, offset=3 * POOL_BYTES + (j + 1) * 1024, align_bytes=64)
+            elif j == 2:
+                result = sb.tile([P, Q], F32, name="result2", tag="turned3", align_bytes=64)
             else:
-                result = sb.tile([P, Q], F32, name="result%d" % j)
-            nc.vector.tensor_tensor(out=result[:], in0=acc[:], in1=recalled, op=MAX)
+                result = sb.tile([P, Q], F32, name="result3")
+            nc.vector.tensor_tensor(out=result[:], in0=acc[:], in1=recalled[:], op=MAX)
             nc.sync.dma_start(out=out[j * P : (j + 1) * P, :], in_=result[:])
 
-        def recall(j, dst):
-            gather(False, dst, memory[j][:], list3[:])
-            return dst
+        def recall(j):
+            if j in {0: POOL_BYTES, 3: 3 * POOL_BYTES + 4096}:
+                recalled = reused.tile([P, Q], F32, name="recalled%d" % j, offset={0: POOL_BYTES, 3: 3 * POOL_BYTES + 4096}[j], align_bytes=64)
+            else:
+                recalled = sb.tile([P, Q], F32, name="recalled%d" % j)
+            gather(j == 0, recalled[:], memory[j][:], list3[:])
+            return recalled
 
-        early = sb.tile([P, 2, Q], F32, name="early")
         turned0 = pick(0)
-        weigh(1, diff1, reused.tile([P, BANK], BF16, name="weights_b1", offset=0, align_bytes=64))
-        rec0 = recall(0, early[:, 0, :])
-        rec1 = recall(1, early[:, 1, :])
+        diff1 = bank(5, [P, PACK, P])
+        turn_add(diff1, second1, True)
+        turn_add(diff1, first1, False)
         turned1 = pick(1)
-        late = sb.tile([P, 2, Q], F32, name="late", tag="listed1")
-        rec2 = recall(2, late[:, 0, :])
-        rec3 = recall(3, late[:, 1, :])
-        acc0 = read(0, turned0)
+        recalled = [recall(j) for j in range(3)]
         turned2 = pick(2)
-        finish(0, acc0, rec0)
-        acc1 = read(1, turned1)
+        weights_b1 = weigh(1, diff1, reused.tile([P, BANK], BF16, name="weights_b1", offset=2 * POOL_BYTES + 1024, align_bytes=64))
+        vals0_mx = quantise_vals(0, turned0)
+        quantise_weights(1, weights_b1)
+        acc0 = read(0, vals0_mx)
+        acc1 = read(1, quantise_vals(1, turned1))
         turned3 = pick(3)
-        acc2 = read(2, turned2)
-        finish(1, acc1, rec1)
-        finish(2, acc2, rec2)
-        finish(3, read(3, turned3), rec3)
+        recalled.append(recall(3))
+        acc2 = read(2, quantise_vals(2, turned2))
+        finish(0, acc0, recalled[0])
+        finish(1, acc1, recalled[1])
+        acc3 = read(3, quantise_vals(3, turned3))
+        finish(2, acc2, recalled[2])
+        finish(3, acc3, recalled[3])

@@ -40,9 +40,9 @@ def tile_attend_difference_memorylarger_lean_kernel(
             nc.sync.dma_start(out=raw[:], in_=src.rearrange("(p j) w -> p j w", j=PACK))
             return raw
 
-        def interleave(name, raw, tag):
+        def interleave(name, raw):
             width = raw.shape[2]
-            grouped = sb.tile([P, width * PACK], BF16, name=name, tag=tag, align_bytes=64)
+            grouped = sb.tile([P, width * PACK], BF16, name=name, align_bytes=64)
             nc.vector.tensor_copy(
                 out=grouped[:].rearrange("p (c i j) -> p c j i", i=4, j=PACK),
                 in_=raw[:].rearrange("p j (c i) -> p c j i", i=4),
@@ -102,9 +102,9 @@ def tile_attend_difference_memorylarger_lean_kernel(
         wm_raw = load_k_first("wm_raw", wm)
         list3 = sb.tile([P, Q // 16], U16, name="list3")
         nc.sync.dma_start(out=list3[:], in_=offs3)
+        store_raw = [load_k_first("store_raw%d" % h, mstore[:, h * BANK : (h + 1) * BANK]) for h in range(2)]
         factor = sb.tile([P, PACK], F32, name="factor")
         nc.sync.dma_start(out=factor[:], in_=slot_factor.rearrange("o (p t) -> (o p) t", t=PACK))
-        store_raw = [load_k_first("store_raw%d" % h, mstore[:, h * BANK : (h + 1) * BANK]) for h in range(2)]
         val_pool = []
         for j in range(4):
             window = reused.tile([P, T], F32, name="val_pool%d" % j, offset=j * POOL_BYTES, align_bytes=64)
@@ -114,7 +114,7 @@ def tile_attend_difference_memorylarger_lean_kernel(
         ident = sb.tile([P, P], F32, name="ident")
         make_identity(nc, ident[:])
 
-        query_mx = quantise("query", interleave("query_b", query_raw, "query_b"))
+        query_mx = quantise("query", interleave("query_b", query_raw))
         scores = [sb.tile([P, T], F32, name="scores%d" % h) for h in range(2)]
         for h in range(2):
             for a in range(4):
@@ -165,23 +165,20 @@ def tile_attend_difference_memorylarger_lean_kernel(
         first1 = sb.tile([P, SLOTS], F32, name="first1")
         gather(False, first1[:], scores[1][:], list1[:])
 
-        wm_mx = quantise("wm", interleave("wm_b", wm_raw, "staged"))
-        remember(0, quantise("store0", interleave("store_b0", store_raw[0], "staged")), (1, 2, 3, 4), ())
-        store_b1 = interleave("store_b1", store_raw[1], "staged")
-        weights_b0 = weigh(0, diff0, sb.tile([P, BANK], BF16, name="weights_b0", tag="store_raw1", align_bytes=64))
-        remember(1, quantise("store1", store_b1), (5, 6, 7, 2), ())
+        wm_mx = quantise("wm", interleave("wm_b", wm_raw))
+        remember(0, quantise("store0", interleave("store_b0", store_raw[0])), (1, 2, 3, 4), ())
+        store_b1 = interleave("store_b1", store_raw[1])
+        weights_b0 = weigh(0, diff0, sb.tile([P, BANK], BF16, name="weights_b0", align_bytes=64))
+        remember(1, quantise("store1", store_b1), (5, 6, 7, 2), (2, 3))
         quantise_weights(0, weights_b0)
 
         def pick(j):
-            if j < 3:
-                listed = sb.tile([P, SLOTS], BF16, name="listed%d" % j, tag=("staged", "store_raw1", "memory0")[j], align_bytes=64)
-            else:
-                listed = reused.tile([P, SLOTS], BF16, name="listed3", offset=2 * POOL_BYTES + 1024, align_bytes=64)
+            listed = sb.tile([P, SLOTS], BF16, name="listed%d" % j)
             if j < 3:
                 gather(True, listed[:], val_pool[j][:], list1[:])
             else:
-                gather(True, listed[:, : 16 * 16], val_pool[j][:], list1[:, :16])
-                gather(False, listed[:, 16 * 16 :], val_pool[j][:], list1[:, 16:])
+                gather(True, listed[:, : 16 * 14], val_pool[j][:], list1[:, :14])
+                gather(False, listed[:, 16 * 14 :], val_pool[j][:], list1[:, 14:])
             pairs = listed[:].bitcast(F32)
             acc = bank((3, 1, 3, 1)[j], [P, 2, P])
             for u in range(2):
@@ -216,11 +213,8 @@ def tile_attend_difference_memorylarger_lean_kernel(
             nc.sync.dma_start(out=out[j * P : (j + 1) * P, :], in_=result[:])
 
         def recall(j):
-            if j in {0: POOL_BYTES, 3: 3 * POOL_BYTES + 4096}:
-                recalled = reused.tile([P, Q], F32, name="recalled%d" % j, offset={0: POOL_BYTES, 3: 3 * POOL_BYTES + 4096}[j], align_bytes=64)
-            else:
-                recalled = sb.tile([P, Q], F32, name="recalled%d" % j)
-            gather(j == 0, recalled[:], memory[j][:], list3[:])
+            recalled = sb.tile([P, Q], F32, name="recalled%d" % j)
+            gather(False, recalled[:], memory[j][:], list3[:])
             return recalled
 
         turned0 = pick(0)
@@ -228,7 +222,7 @@ def tile_attend_difference_memorylarger_lean_kernel(
         turn_add(diff1, second1, True)
         turn_add(diff1, first1, False)
         turned1 = pick(1)
-        recalled = [recall(j) for j in range(3)]
+        recalled = [recall(j) for j in range(4)]
         turned2 = pick(2)
         weights_b1 = weigh(1, diff1, reused.tile([P, BANK], BF16, name="weights_b1", offset=2 * POOL_BYTES + 1024, align_bytes=64))
         vals0_mx = quantise_vals(0, turned0)
@@ -236,7 +230,6 @@ def tile_attend_difference_memorylarger_lean_kernel(
         acc0 = read(0, vals0_mx)
         acc1 = read(1, quantise_vals(1, turned1))
         turned3 = pick(3)
-        recalled.append(recall(3))
         acc2 = read(2, quantise_vals(2, turned2))
         finish(0, acc0, recalled[0])
         finish(1, acc1, recalled[1])

@@ -40,14 +40,25 @@ def tile_attend_difference_memorylarger_lean_kernel(
             nc.sync.dma_start(out=raw[:], in_=src.rearrange("(p j) w -> p j w", j=PACK))
             return raw
 
-        def interleave(name, raw):
+        def interleave(name, raw, on_vector=True):
             width = raw.shape[2]
             grouped = sb.tile([P, width * PACK], BF16, name=name, align_bytes=64)
-            nc.vector.tensor_copy(
-                out=grouped[:].rearrange("p (c i j) -> p c j i", i=4, j=PACK),
-                in_=raw[:].rearrange("p j (c i) -> p c j i", i=4),
-            )
+            dst = grouped[:].rearrange("p (c i j) -> p c j i", i=4, j=PACK)
+            src = raw.rearrange("p j (c i) -> p c j i", i=4)
+            if on_vector:
+                nc.vector.tensor_copy(out=dst, in_=src)
+            else:
+                nc.scalar.copy(out=dst, in_=src)
             return grouped
+
+        def quantise_in_halves(name, raw, second_on_vector=True):
+            half = raw.shape[2] // 2
+            codes, scales = mx_tiles(name, 2 * half)
+            parts = [interleave("%s_b%d" % (name, x), raw[:, :, x * half : (x + 1) * half], x == 0 or second_on_vector) for x in range(2)]
+            for x in range(2):
+                cols = slice(x * half, (x + 1) * half)
+                quantise_into(codes[:, cols], scales[:, cols], parts[x][:])
+            return codes, scales
 
         def mx_tiles(name, width):
             codes = sb.tile([P, width], U32, name=name + "_codes", align_bytes=64)
@@ -114,7 +125,7 @@ def tile_attend_difference_memorylarger_lean_kernel(
         ident = sb.tile([P, P], F32, name="ident")
         make_identity(nc, ident[:])
 
-        query_mx = quantise("query", interleave("query_b", query_raw))
+        query_mx = quantise_in_halves("query", query_raw)
         scores = [sb.tile([P, T], F32, name="scores%d" % h) for h in range(2)]
         for h in range(2):
             for a in range(4):
@@ -165,9 +176,9 @@ def tile_attend_difference_memorylarger_lean_kernel(
         first1 = sb.tile([P, SLOTS], F32, name="first1")
         gather(False, first1[:], scores[1][:], list1[:])
 
-        wm_mx = quantise("wm", interleave("wm_b", wm_raw))
-        remember(0, quantise("store0", interleave("store_b0", store_raw[0])), (1, 2, 3, 4), ())
-        store_b1 = interleave("store_b1", store_raw[1])
+        wm_mx = quantise_in_halves("wm", wm_raw)
+        remember(0, quantise_in_halves("store0", store_raw[0]), (1, 2, 3, 4), ())
+        store_b1 = interleave("store_b1", store_raw[1][:])
         weights_b0 = weigh(0, diff0, sb.tile([P, BANK], BF16, name="weights_b0", align_bytes=64))
         remember(1, quantise("store1", store_b1), (5, 6, 7, 2), (2, 3))
         quantise_weights(0, weights_b0)
@@ -213,7 +224,10 @@ def tile_attend_difference_memorylarger_lean_kernel(
             nc.sync.dma_start(out=out[j * P : (j + 1) * P, :], in_=result[:])
 
         def recall(j):
-            recalled = sb.tile([P, Q], F32, name="recalled%d" % j)
+            if j in {3: 3 * POOL_BYTES + 4096}:
+                recalled = reused.tile([P, Q], F32, name="recalled%d" % j, offset={3: 3 * POOL_BYTES + 4096}[j], align_bytes=64)
+            else:
+                recalled = sb.tile([P, Q], F32, name="recalled%d" % j)
             gather(False, recalled[:], memory[j][:], list3[:])
             return recalled
 
@@ -222,7 +236,7 @@ def tile_attend_difference_memorylarger_lean_kernel(
         turn_add(diff1, second1, True)
         turn_add(diff1, first1, False)
         turned1 = pick(1)
-        recalled = [recall(j) for j in range(4)]
+        recalled = [recall(j) for j in range(3)]
         turned2 = pick(2)
         weights_b1 = weigh(1, diff1, reused.tile([P, BANK], BF16, name="weights_b1", offset=2 * POOL_BYTES + 1024, align_bytes=64))
         vals0_mx = quantise_vals(0, turned0)
@@ -230,6 +244,7 @@ def tile_attend_difference_memorylarger_lean_kernel(
         acc0 = read(0, vals0_mx)
         acc1 = read(1, quantise_vals(1, turned1))
         turned3 = pick(3)
+        recalled.append(recall(3))
         acc2 = read(2, quantise_vals(2, turned2))
         finish(0, acc0, recalled[0])
         finish(1, acc1, recalled[1])

from contextlib import ExitStack

import concourse.mybir as mybir
from concourse.masks import make_identity

D, T, SLOTS, Q, E, M, C = 512, 2048, 512, 256, 512, 1024, 512
FLOPS = 2 * (Q * D * T + E * SLOTS * Q + E * C * M)

F32 = mybir.dt.float32
BF16 = mybir.dt.bfloat16
I32 = mybir.dt.int32
U32 = mybir.dt.uint32
U16 = mybir.dt.uint16
U8 = mybir.dt.uint8
FP8X4 = mybir.dt.float8_e4m3fn_x4
COPY = mybir.ActivationFunctionType.Copy
MAX = mybir.AluOpType.max
MULT = mybir.AluOpType.mult

P = 128
PACK = 4
BANK = 512
POOL_BYTES = T * 4


def tile_attend_difference_memorylarger_lean_kernel(
    tc, query, keys_words, keys_scales, slot_factor, vals, wm, mstore, offs, offs2, offs3, out
):
    nc = tc.nc
    with ExitStack() as ctx:
        sb = ctx.enter_context(tc.tile_pool(name="sb", bufs=1))
        reused = ctx.enter_context(tc.tile_pool(name="reused", bufs=1))
        ps = ctx.enter_context(tc.psum_pool(name="ps", bufs=1))

        def bank(b, shape):
            return ps.tile(shape, F32, name="bank%d" % b)

        def load_k_first(name, src):
            raw = sb.tile([P, PACK, src.shape[1]], F32, name=name, align_bytes=64)
            nc.sync.dma_start(out=raw[:], in_=src.rearrange("(p j) w -> p j w", j=PACK))
            return raw

        def interleave(name, raw, on_vector=True):
            width = raw.shape[2]
            grouped = sb.tile([P, width * PACK], BF16, name=name, align_bytes=64)
            dst = grouped[:].rearrange("p (c i j) -> p c j i", i=4, j=PACK)
            src = raw.rearrange("p j (c i) -> p c j i", i=4)
            if on_vector:
                nc.vector.tensor_copy(out=dst, in_=src)
            else:
                nc.scalar.copy(out=dst, in_=src)
            return grouped

        def quantise_in_halves(name, raw, second_on_vector=True):
            half = raw.shape[2] // 2
            codes, scales = mx_tiles(name, 2 * half)
            parts = [interleave("%s_b%d" % (name, x), raw[:, :, x * half : (x + 1) * half], x == 0 or second_on_vector) for x in range(2)]
            for x in range(2):
                cols = slice(x * half, (x + 1) * half)
                quantise_into(codes[:, cols], scales[:, cols], parts[x][:])
            return codes, scales

        def mx_tiles(name, width):
            codes = sb.tile([P, width], U32, name=name + "_codes", align_bytes=64)
            scales = sb.tile([P, width], U8, name=name + "_scales", align_bytes=64)
            return codes, scales

        def quantise_into(codes, scales, grouped):
            nc.vector.quantize_mx(out=codes.bitcast(FP8X4), scales=scales, in_=grouped)

        def quantise(name, grouped):
            codes, scales = mx_tiles(name, grouped.shape[1] // PACK)
            quantise_into(codes[:], scales[:], grouped[:])
            return codes, scales

        def product(dst, left, cols, right_codes, right_scales):
            nc.tensor.matmul_mx(
                out=dst, lhsT=left[0][:, cols].bitcast(FP8X4), lhsT_scale=left[1][:, cols],
                rhs=right_codes.bitcast(FP8X4), rhs_scale=right_scales, start=True, stop=True,
            )

        def leave_psum(on_vector, dst, src):
            if on_vector:
                nc.vector.tensor_copy(out=dst, in_=src)
            else:
                nc.scalar.copy(out=dst, in_=src)

        def gather(on_vector, dst, window, offsets):
            if on_vector:
                nc.vector.tensor_copy(out=dst, in_=window.indirect(offsets))
            else:
                nc.scalar.activation(out=dst, in_=window.indirect(offsets), func=COPY)

        key_scales = sb.tile([P, BANK], U8, name="key_scales", align_bytes=64)
        nc.vector.memset(key_scales[:].bitcast(I32), 0)
        query_raw = load_k_first("query_raw", query)
        scale_words = keys_scales[0].bitcast(I32)
        for quad in range(4):
            nc.sync.dma_start(
                out=key_scales[32 * quad : 32 * quad + 16, :].bitcast(I32),
                in_=scale_words[4 * quad : 4 * quad + 4, :].rearrange("r (a c) -> a r c", a=4),
            )
        key_words = keys_words[0].rearrange("p n t -> p (n t)").bitcast(I32)
        key_codes = []
        for half in range(2):
            codes = sb.tile([P, T // 2], U32, name="key_codes%d" % half, align_bytes=64)
            nc.sync.dma_start(out=codes[:].bitcast(I32), in_=key_words[:, half * (T // 2) : (half + 1) * (T // 2)])
            key_codes.append(codes)
        list2 = sb.tile([P, SLOTS // 16], U16, name="list2")
        nc.sync.dma_start(out=list2[:], in_=offs2)
        list1 = sb.tile([P, SLOTS // 16], U16, name="list1")
        nc.sync.dma_start(out=list1[:], in_=offs)
        wm_raw = load_k_first("wm_raw", wm)
        list3 = sb.tile([P, Q // 16], U16, name="list3")
        nc.sync.dma_start(out=list3[:], in_=offs3)
        store_raw = [load_k_first("store_raw%d" % h, mstore[:, h * BANK : (h + 1) * BANK]) for h in range(2)]
        factor = sb.tile([P, PACK], F32, name="factor")
        nc.sync.dma_start(out=factor[:], in_=slot_factor.rearrange("o (p t) -> (o p) t", t=PACK))
        val_pool = []
        for j in range(4):
            window = reused.tile([P, T], F32, name="val_pool%d" % j, offset=j * POOL_BYTES, align_bytes=64)
            nc.sync.dma_start(out=window[:], in_=vals[j * P : (j + 1) * P, :])
            val_pool.append(window)

        ident = sb.tile([P, P], F32, name="ident")
        make_identity(nc, ident[:])

        query_mx = quantise_in_halves("query", query_raw)
        scores = [sb.tile([P, T], F32, name="scores%d" % h) for h in range(2)]
        for h in range(2):
            for a in range(4):
                acc = bank(4 * h + a, [P, BANK])
                product(acc[:], query_mx, slice(h * P, (h + 1) * P),
                        key_codes[a // 2][:, (a % 2) * BANK : (a % 2 + 1) * BANK], key_scales[4 * a :, :])
                leave_psum(4 * h + a in (1, 3, 5), scores[h][:, a * BANK : (a + 1) * BANK], acc[:])

        def negated_second(h):
            second = sb.tile([P, SLOTS], F32, name="second%d" % h)
            nc.scalar.activation(out=second[:], in_=scores[h][:].indirect(list2[:]), func=COPY, scale=-1.0)
            return second

        def turn_add(acc, src, opens):
            for t in range(PACK):
                nc.tensor.matmul(out=acc[:, t, :], lhsT=src[:, t::PACK], rhs=ident[:], is_transpose=True,
                                 start=(opens and t == 0), stop=(not opens and t == PACK - 1))

        weights_mx = mx_tiles("weights", Q)

        def weigh(h, diff, grouped):
            nc.vector.scalar_tensor_tensor(
                out=grouped[:].rearrange("p (q t) -> p q t", t=PACK),
                in0=diff[:].rearrange("p t q -> p q t"), scalar=0.0,
                in1=factor[:].unsqueeze(1).to_broadcast([P, P, PACK]), op0=MAX, op1=MULT,
            )
            return grouped

        def quantise_weights(h, grouped):
            cols = slice(h * P, (h + 1) * P)
            quantise_into(weights_mx[0][:, cols], weights_mx[1][:, cols], grouped[:])

        memory = [sb.tile([P, M], F32, name="memory%d" % j, align_bytes=64) for j in range(4)]

        def remember(h, store_mx, banks, on_vector):
            for j in range(4):
                acc = bank(banks[j], [P, BANK])
                product(acc[:], wm_mx, slice(j * P, (j + 1) * P), store_mx[0][:], store_mx[1][:])
                leave_psum(j in on_vector, memory[j][:, h * BANK : (h + 1) * BANK], acc[:])

        second0 = negated_second(0)
        diff0 = bank(0, [P, PACK, P])
        turn_add(diff0, second0, True)
        first0 = sb.tile([P, SLOTS], F32, name="first0")
        gather(False, first0[:], scores[0][:], list1[:])
        turn_add(diff0, first0, False)
        second1 = negated_second(1)
        first1 = sb.tile([P, SLOTS], F32, name="first1")
        gather(False, first1[:], scores[1][:], list1[:])

        wm_mx = quantise_in_halves("wm", wm_raw)
        remember(0, quantise_in_halves("store0", store_raw[0]), (1, 2, 3, 4), ())
        store_b1 = interleave("store_b1", store_raw[1][:])
        weights_b0 = weigh(0, diff0, sb.tile([P, BANK], BF16, name="weights_b0", align_bytes=64))
        remember(1, quantise("store1", store_b1), (5, 6, 7, 2), (2, 3))
        quantise_weights(0, weights_b0)

        def pick(j):
            listed = sb.tile([P, SLOTS], BF16, name="listed%d" % j)
            if j < 3:
                gather(True, listed[:], val_pool[j][:], list1[:])
            else:
                gather(True, listed[:, : 16 * 14], val_pool[j][:], list1[:, :14])
                gather(False, listed[:, 16 * 14 :], val_pool[j][:], list1[:, 14:])
            pairs = listed[:].bitcast(F32)
            acc = bank((3, 1, 3, 1)[j], [P, 2, P])
            for u in range(2):
                nc.tensor.transpose(acc[:, u, :], pairs[:, u::2], ident[:])
            turned = sb.tile([P, P * PACK], BF16, name="turned%d" % j, align_bytes=64)
            nc.scalar.copy(out=turned[:].bitcast(F32).rearrange("p (e u) -> p e u", u=2),
                           in_=acc[:].rearrange("p u e -> p e u"))
            return turned

        def quantise_vals(j, turned):
            if j < 3:
                codes = reused.tile([P, P], U32, name="vals_codes%d" % j, offset=(2 * POOL_BYTES + 2048, 2 * POOL_BYTES, 3 * POOL_BYTES)[j], align_bytes=64)
            else:
                codes = sb.tile([P, P], U32, name="vals_codes3", align_bytes=64)
            scales = sb.tile([P, P], U8, name="vals_scales%d" % j, align_bytes=64)
            quantise_into(codes[:], scales[:], turned[:])
            return codes, scales

        def read(j, vals_mx):
            acc = bank((0, 4, 6, 7)[j], [P, Q])
            product(acc[:], vals_mx, slice(0, P), weights_mx[0][:], weights_mx[1][:])
            return acc

        def finish(j, acc, recalled):
            if j < 2:
                result = reused.tile([P, Q], F32, name="result%d" % j, offset=3 * POOL_BYTES + (j + 1) * 1024, align_bytes=64)
            elif j == 2:
                result = sb.tile([P, Q], F32, name="result2", tag="turned3", align_bytes=64)
            else:
                result = sb.tile([P, Q], F32, name="result3")
            nc.vector.tensor_tensor(out=result[:], in0=acc[:], in1=recalled[:], op=MAX)
            nc.sync.dma_start(out=out[j * P : (j + 1) * P, :], in_=result[:])

        def recall(j):
            if j in {3: 3 * POOL_BYTES + 4096}:
                recalled = reused.tile([P, Q], F32, name="recalled%d" % j, offset={3: 3 * POOL_BYTES + 4096}[j], align_bytes=64)
            else:
                recalled = sb.tile([P, Q], F32, name="recalled%d" % j)
            gather(False, recalled[:], memory[j][:], list3[:])
            return recalled

        turned0 = pick(0)
        diff1 = bank(5, [P, PACK, P])
        turn_add(diff1, second1, True)
        turn_add(diff1, first1, False)
        turned1 = pick(1)
        recalled = [recall(j) for j in range(3)]
        turned2 = pick(2)
        weights_b1 = weigh(1, diff1, reused.tile([P, BANK], BF16, name="weights_b1", offset=2 * POOL_BYTES + 1024, align_bytes=64))
        vals0_mx = quantise_vals(0, turned0)
        quantise_weights(1, weights_b1)
        acc0 = read(0, vals0_mx)
        acc1 = read(1, quantise_vals(1, turned1))
        turned3 = pick(3)
        recalled.append(recall(3))
        acc2 = read(2, quantise_vals(2, turned2))
        finish(0, acc0, recalled[0])
        finish(1, acc1, recalled[1])
        acc3 = read(3, quantise_vals(3, turned3))
        finish(2, acc2, recalled[2])
        finish(3, acc3, recalled[3])
